import numpy as np
import ml_dtypes


def mxq(x, axis, fmt="e4m3"):
    dtype, down = {"e4m3": (ml_dtypes.float8_e4m3fn, 7), "e5m2": (ml_dtypes.float8_e5m2, 14)}[fmt]
    v = np.moveaxis(np.asarray(x, np.float32).astype(ml_dtypes.bfloat16).astype(np.float64), axis, -1)
    blocks = v.reshape(v.shape[:-1] + (-1, 32))
    amax = np.abs(blocks).max(-1, keepdims=True)
    byte = np.maximum(np.where(amax > 0, np.frexp(amax)[1] - 1 + 127, 0) - down, 1)
    scale = np.exp2(byte - 127.0)
    codes = (blocks / scale).astype(np.float32).astype(dtype).astype(np.float64)
    return np.moveaxis((codes * scale).reshape(v.shape), -1, axis)


WIDE = False


def mx_kscale(k):
    if not WIDE:
        return np.ones(k)
    levels = np.array([10, -10, 5, -5, 0])
    if k % 512:
        return np.exp2(np.random.permutation(np.resize(levels, k // 32))).repeat(32)
    a = np.empty((k // 512, 16))
    for p in range(k // 512):
        a[p, :8] = np.random.permutation(np.resize(levels, 8))
        for g in range(8):
            far = levels[np.abs(levels - a[p, g]) >= 10]
            a[p, g + 8] = far[np.random.randint(len(far))]
    return np.exp2(a.ravel()).repeat(32)


def f64(x):
    return np.asarray(x).astype(np.float64)


def striped(idx):
    return np.tile(idx.reshape(-1, 16).T, (8, 1)).astype(np.uint16)


def unstriped(offs):
    return offs[:16].T.reshape(-1).astype(np.int64)


E2M1 = np.array([0.0, 0.5, 1.0, 1.5, 2.0, 3.0, 4.0, 6.0, -0.0, -0.5, -1.0, -1.5, -2.0, -3.0, -4.0, -6.0])


def pack_weight(w, fmt):
    k, n = w.shape
    w = f64(np.asarray(w, np.float32).astype(ml_dtypes.bfloat16)).reshape(k // 32, 32, n)
    amax = np.abs(w).max(1)
    if fmt == "e4m3":
        byte = np.frexp(amax)[1] - 1 + 127 - 7
    else:
        mant, ex = np.frexp(amax / 6.0)
        byte = np.where(mant > 0.5, ex, ex - 1) + 127
    byte = np.clip(np.where(amax > 0, byte, 1), 1, 254)
    scaled = (w * np.exp2(127.0 - byte)[:, None, :]).reshape(k, n).astype(np.float32)
    by_word = np.ascontiguousarray(scaled.reshape(k // 512, 128, 4, n).transpose(0, 1, 3, 2))
    if fmt == "e4m3":
        words = by_word.astype(ml_dtypes.float8_e4m3fn).view(np.uint8)
    else:
        c = by_word.astype(ml_dtypes.float4_e2m1fn).view(np.uint8) & 0xF
        words = (c[..., 0::2] | (c[..., 1::2] << 4)).reshape(k // 512, 128, 2 * n)
    return np.ascontiguousarray(words), np.ascontiguousarray(byte.astype(np.uint8).reshape(k // 512, 16, n))


def unpack_weight(words, scales, fmt):
    g, _, n = scales.shape
    words = np.ascontiguousarray(words).reshape(g, 128, n, -1)
    if fmt == "e4m3":
        vals = words.view(ml_dtypes.float8_e4m3fn).astype(np.float64)
    else:
        nib = np.empty((g, 128, n, 4), np.uint8)
        nib[..., 0::2] = words & 0xF
        nib[..., 1::2] = words >> 4
        vals = E2M1[nib]
    vals = vals * np.repeat(np.exp2(scales.astype(np.float64) - 127.0), 8, axis=1)[..., None]
    return vals.transpose(0, 1, 3, 2).reshape(g * 512, n)


def gelu(v):
    return 0.5 * v * (1.0 + np.tanh(np.sqrt(2.0 / np.pi) * (v + 0.044715 * v**3)))


K, K2, H, N, T, T2, S, P = 512, 1024, 1024, 384, 4096, 2048, 1024, 512

def setup_inputs():
    n = np.random.standard_normal
    s, s2, u = mx_kscale(K)[:, None], mx_kscale(K2)[:, None], mx_kscale(H)[:, None]
    d = {}
    d["tab_words"], d["tab_scales"] = pack_weight(n((K, T)) * s, "e4m3")
    d["tab2_words"], d["tab2_scales"] = pack_weight(n((K2, T2)) * s2, "e4m3")
    d["offs"] = striped(np.random.permutation(T)[:S])
    d["offs2"] = striped(np.random.permutation(T2)[:P])
    d["pos1"] = striped(np.random.permutation(S)[:P])
    d["w1"] = (n((K, H)) / K**0.5 / s * u.T).astype(np.float32)
    d["res"] = (0.7 * n((H, S)) * u).astype(np.float32)
    d["w2_words"], d["w2_scales"] = pack_weight(n((K2, H)) / K2**0.5 / s2, "e2m1")
    d["gain"] = (np.exp(0.3 * n(H)) * u[:, 0]).astype(np.float32)
    d["wgs"] = np.exp(0.3 * n((128, P))).astype(np.float32)
    d["w3"] = (0.6 * n((H, N)) / H**0.5 / u).astype(np.float32)
    d["w4_words"], d["w4_scales"] = pack_weight(0.7 * n((H, N)) / H**0.5 / u, "e4m3")
    return d

def reference(tab_words, tab_scales, tab2_words, tab2_scales, offs, offs2, pos1, w1, res, w2_words, w2_scales, gain, wgs, w3, w4_words, w4_scales):
    v = unpack_weight(tab_words, tab_scales, "e4m3")[:, unstriped(offs)]
    v2 = unpack_weight(tab2_words, tab2_scales, "e4m3")[:, unstriped(offs2)]
    w2 = unpack_weight(w2_words, w2_scales, "e2m1")
    w4 = unpack_weight(w4_words, w4_scales, "e4m3")
    a = (mxq(f64(w1), 0, "e4m3").T @ v) + f64(res)
    x = w2.T @ v2
    b = 0.5 * x * (1.0 + np.tanh(np.sqrt(2.0 / np.pi) * (x + 0.044715 * x**3)))
    b = b * f64(gain)[:, None]
    placed = np.zeros((H, S))
    placed[:, unstriped(pos1)] = np.tile(f64(wgs), (H // 128, 1)) * b
    z = np.maximum(a, placed)
    y = mxq(f64(w3), 0, "e4m3").T @ mxq(z, 0, "e4m3")
    f = w4.T @ mxq(placed, 0, "e4m3")
    return y + np.sin(f)

@@ -1,0 +1,254 @@
+import math
+from contextlib import ExitStack
+
+import concourse.mybir as mybir
+
+K, K2, H, N, T, T2, S, PICKS = 512, 1024, 1024, 384, 4096, 2048, 1024, 512
+FLOPS = 2 * (K * H * S + K2 * H * PICKS + 2 * H * N * S)
+
+F32 = mybir.dt.float32
+BF16 = mybir.dt.bfloat16
+I32 = mybir.dt.int32
+U32 = mybir.dt.uint32
+U16 = mybir.dt.uint16
+U8 = mybir.dt.uint8
+FP8X4 = mybir.dt.float8_e4m3fn_x4
+FP4X4 = mybir.dt.float4_e2m1fn_x4
+ALU = mybir.AluOpType
+ACT = mybir.ActivationFunctionType
+
+P = 128
+PACK = 4
+PASS = P * PACK
+BANK = 512
+QUADS = 4
+LINE = 4
+
+
+def tile_list_song_rotation_scorer_kernel(
+    tc, tab_words, tab_scales, tab2_words, tab2_scales, offs, offs2, pos1, w1, res,
+    w2_words, w2_scales, gain, wgs, w3, w4_words, w4_scales, out,
+):
+    nc = tc.nc
+    r_passes = H // PASS
+    halves = S // BANK
+    n_tiles = N // P
+
+    with ExitStack() as ctx:
+        keep = ctx.enter_context(tc.tile_pool(name="keep", bufs=1))
+        ring = ctx.enter_context(tc.tile_pool(name="ring", bufs=2))
+        psum = ctx.enter_context(tc.psum_pool(name="psum", bufs=2))
+
+        def load_scale_rows(planes, scales):
+            for q in range(QUADS):
+                nc.sync.dma_start(
+                    out=planes[32 * q : 32 * q + 4, :, :].bitcast(I32),
+                    in_=scales[:, 4 * q : 4 * q + 4, :].rearrange("a r c -> r a c").bitcast(I32),
+                )
+
+        def zeroed_planes(name, passes, width):
+            planes = keep.tile([P, passes, width], U8, name=name, align_bytes=64)
+            nc.vector.memset(planes[:].rearrange("p a c -> p (a c)").bitcast(I32), 0)
+            return planes
+
+        def load_words(name, words):
+            width = words.shape[1]
+            tile = keep.tile([P, width], I32, name=name, align_bytes=64)
+            nc.sync.dma_start(out=tile[:], in_=words.rearrange("p c i -> p (c i)").bitcast(I32))
+            return tile
+
+        def quantise(codes, scales, grouped):
+            nc.vector.quantize_mx(out=codes.bitcast(FP8X4), scales=scales, in_=grouped)
+
+        def woven(ap):
+            return ap.rearrange("p (c i t) -> p c t i", i=LINE, t=PACK)
+
+        def by_rows(ap):
+            return ap.rearrange("p t (c i) -> p c t i", i=LINE)
+
+        w2_planes = zeroed_planes("w2_planes", 2, H)
+        tab2_planes = zeroed_planes("tab2_planes", 2, T2)
+        tab_planes = zeroed_planes("tab_planes", 1, T)
+        w4_planes = zeroed_planes("w4_planes", r_passes, N)
+        pages = [keep.tile([P, S], F32, name=f"page{t}") for t in range(PACK)]
+        for page in pages:
+            nc.vector.memset(page[:], 0.0)
+
+        idx2 = keep.tile([P, PICKS // 16], U16, name="idx2")
+        nc.sync.dma_start(idx2[:], offs2)
+        w2_raw = keep.tile([P, 2, H], U16, name="w2_raw", align_bytes=64)
+        nc.sync.dma_start(out=w2_raw[:].bitcast(I32), in_=w2_words.rearrange("a p c -> p a c").bitcast(I32))
+        load_scale_rows(w2_planes, w2_scales)
+        tab2_w = [load_words(f"tab2_w{a}", tab2_words[a]) for a in range(2)]
+        load_scale_rows(tab2_planes, tab2_scales)
+        slots = keep.tile([P, PICKS // 16], U16, name="slots")
+        nc.sync.dma_start(slots[:], pos1)
+        weights = keep.tile([P, PACK, PICKS], F32, name="weights")
+        for q in range(QUADS):
+            nc.sync.dma_start(out=weights[32 * q : 32 * q + 32, :, :], in_=wgs.rearrange("(p t) j -> p t j", t=PACK))
+        gains = keep.tile([P, r_passes, PACK], F32, name="gains")
+        nc.sync.dma_start(out=gains[:], in_=gain.rearrange("(b p t) -> p b t", p=P, t=PACK))
+        idx = keep.tile([P, S // 16], U16, name="idx")
+        nc.sync.dma_start(idx[:], offs)
+        tab_w = load_words("tab_w", tab_words[0])
+        load_scale_rows(tab_planes, tab_scales)
+        w1_raw = ring.tile([P, PACK, H], F32, name="w1_raw", tag="rows16k")
+        nc.sync.dma_start(out=w1_raw[:], in_=w1.rearrange("(p j) c -> p j c", j=PACK))
+        feats = []
+        for b in range(r_passes):
+            feat = keep.tile([P, PACK, S], F32, name=f"feat{b}")
+            nc.sync.dma_start(out=feat[:], in_=res[b * PASS : (b + 1) * PASS, :].rearrange("(p t) j -> p t j", t=PACK))
+            feats.append(feat)
+        w4_codes = keep.tile([P, r_passes, N], I32, name="w4_codes", align_bytes=64)
+        nc.sync.dma_start(out=w4_codes[:], in_=w4_words.rearrange("a p c i -> p a (c i)").bitcast(I32))
+        load_scale_rows(w4_planes, w4_scales)
+
+        w2_codes = keep.tile([P, 2, H], U16, name="w2_codes", align_bytes=64)
+        nc.vector.tensor_copy(
+            out=w2_codes[:].rearrange("p a (b t m) -> p (a b) m t", t=PACK, m=P),
+            in_=w2_raw[:].rearrange("p a (b m t) -> p (a b) m t", t=PACK, m=P),
+        )
+        w2_dealt = keep.tile([P, 2, H], U8, name="w2_dealt", align_bytes=64)
+        nc.vector.tensor_copy(
+            out=w2_dealt[:].rearrange("p a (b t m) -> p (a b) m t", t=PACK, m=P),
+            in_=w2_planes[:].rearrange("p a (b m t) -> p (a b) m t", t=PACK, m=P),
+        )
+
+        v2_codes = keep.tile([P, 2, PICKS], U32, name="v2_codes", align_bytes=64)
+        v2_scales = keep.tile([P, 2, PICKS], U8, name="v2_scales", align_bytes=64)
+        for a in range(2):
+            nc.vector.tensor_copy(v2_codes[:, a, :], tab2_w[a][:].bitcast(U32).indirect(idx2[:]))
+        for a in range(2):
+            nc.vector.tensor_copy(v2_scales[:, a, :], tab2_planes[:, a, :].indirect(idx2[:]))
+
+        w1_codes = keep.tile([P, H], U32, name="w1_codes", align_bytes=64)
+        w1_scales = keep.tile([P, H], U8, name="w1_scales", align_bytes=64)
+
+        def quantise_w1():
+            for b in range(r_passes):
+                cols = slice(b * PASS, (b + 1) * PASS)
+                grouped = ring.tile([P, PACK * BANK], BF16, name="grouped", bufs=4, align_bytes=64)
+                nc.scalar.copy(
+                    out=grouped[:].rearrange("p (t m j) -> p m j t", t=PACK, j=PACK),
+                    in_=w1_raw[:, :, cols].rearrange("p j (m t) -> p m j t", t=PACK),
+                )
+                quantise(w1_codes[:, cols], w1_scales[:, cols], grouped[:])
+
+        placed = []
+        for b in range(r_passes):
+            if b == 1:
+                quantise_w1()
+            placed_b = ring.tile([P, PACK, S], F32, name=f"placed{b}", tag="rows16k")
+            placed.append(placed_b)
+            for t in range(PACK):
+                cols = slice(b * PASS + t * P, b * PASS + (t + 1) * P)
+                x = psum.tile([P, PICKS], F32, name="x")
+                for a in range(2):
+                    nc.tensor.matmul_mx(
+                        out=x[:],
+                        lhsT=w2_codes[:, a, cols].bitcast(FP4X4),
+                        lhsT_scale=w2_dealt[:, a, cols],
+                        rhs=v2_codes[:, a, :].bitcast(FP8X4),
+                        rhs_scale=v2_scales[:, a, :],
+                        start=(a == 0),
+                        stop=(a == 1),
+                    )
+                act = ring.tile([P, PICKS], F32, name="act", bufs=3)
+                nc.scalar.activation(out=act[:], in_=x[:], func=ACT.Gelu_apprx_tanh)
+                nc.vector.tensor_tensor(pages[t][:].indirect(slots[:]), act[:], weights[:, t, :], ALU.mult)
+                nc.scalar.activation(out=placed_b[:, t, :], in_=pages[t][:], func=ACT.Copy, scale=gains[:, b, t : t + 1])
+
+        v_codes = keep.tile([P, S], U32, name="v_codes", align_bytes=64)
+        v_scales = keep.tile([P, S], U8, name="v_scales", align_bytes=64)
+        nc.vector.tensor_copy(v_codes[:], tab_w[:].bitcast(U32).indirect(idx[:]))
+        nc.vector.tensor_copy(v_scales[:], tab_planes[:, 0, :].indirect(idx[:]))
+
+        for b in range(r_passes):
+            for h in range(halves):
+                for t in range(PACK):
+                    cols = slice(b * PASS + t * P, b * PASS + (t + 1) * P)
+                    js = slice(h * BANK, (h + 1) * BANK)
+                    acc = psum.tile([P, BANK], F32, name="acc")
+                    nc.tensor.matmul_mx(
+                        out=acc[:],
+                        lhsT=w1_codes[:, cols].bitcast(FP8X4),
+                        lhsT_scale=w1_scales[:, cols],
+                        rhs=v_codes[:, js].bitcast(FP8X4),
+                        rhs_scale=v_scales[:, js],
+                        start=True,
+                        stop=True,
+                    )
+                    nc.vector.tensor_tensor(feats[b][:, t, js], acc[:], feats[b][:, t, js], ALU.add)
+
+        w3_codes = keep.tile([P, r_passes, N], U32, name="w3_codes", align_bytes=64)
+        w3_scales = keep.tile([P, r_passes, N], U8, name="w3_scales", align_bytes=64)
+        for b in range(r_passes):
+            w3_raw = keep.tile([P, PACK, N], F32, name="w3_raw")
+            nc.sync.dma_start(out=w3_raw[:], in_=w3[b * PASS : (b + 1) * PASS, :].rearrange("(p t) n -> p t n", t=PACK))
+            grouped = ring.tile([P, PACK * BANK], BF16, name="grouped", bufs=4, align_bytes=64)
+            nc.scalar.copy(out=woven(grouped[:, : PACK * N]), in_=by_rows(w3_raw[:]))
+            for lo, hi in ((0, 256), (256, N)):
+                quantise(w3_codes[:, b, lo:hi], w3_scales[:, b, lo:hi], grouped[:, PACK * lo : PACK * hi])
+
+        def second_stage(name, w_codes, w_scales, codes, scales, nt, h):
+            acc = psum.tile([P, BANK], F32, name=name)
+            ns = slice(nt * P, (nt + 1) * P)
+            for b in range(r_passes):
+                nc.tensor.matmul_mx(
+                    out=acc[:],
+                    lhsT=w_codes[:, b, ns].bitcast(FP8X4),
+                    lhsT_scale=w_scales[:, b, ns],
+                    rhs=codes[b][h][:].bitcast(FP8X4),
+                    rhs_scale=scales[b][h][:],
+                    start=(b == 0),
+                    stop=(b == r_passes - 1),
+                )
+            return acc
+
+        def code_tiles(name, dtype):
+            return [
+                [keep.tile([P, BANK], dtype, name=f"{name}{b}{h}", align_bytes=64) for h in range(halves)]
+                for b in range(r_passes)
+            ]
+
+        p_codes, p_scales = code_tiles("p_codes", U32), code_tiles("p_scales", U8)
+        z_codes, z_scales = code_tiles("z_codes", U32), code_tiles("z_scales", U8)
+
+        def quantise_placed(b, h):
+            grouped = ring.tile([P, PACK * BANK], BF16, name="grouped", bufs=4, align_bytes=64)
+            nc.scalar.copy(out=woven(grouped[:]), in_=by_rows(placed[b][:, :, h * BANK : (h + 1) * BANK]))
+            quantise(p_codes[b][h][:], p_scales[b][h][:], grouped[:])
+
+        def merge(b, h):
+            js = slice(h * BANK, (h + 1) * BANK)
+            grouped = ring.tile([P, PACK * BANK], BF16, name="grouped", bufs=4, align_bytes=64)
+            nc.vector.tensor_tensor(woven(grouped[:]), by_rows(feats[b][:, :, js]), by_rows(placed[b][:, :, js]), ALU.max)
+            return grouped
+
+        def sine(nt, h):
+            f = second_stage("f", w4_codes, w4_planes, p_codes, p_scales, nt, h)
+            turns = ring.tile([P, BANK], F32, name="turns")
+            nc.scalar.activation(out=turns[:], in_=f[:], func=ACT.Abs, scale=1.0 / (2.0 * math.pi), bias=-0.25)
+            whole = ring.tile([P, BANK], U32, name="whole")
+            nc.scalar.activation(out=whole[:], in_=turns[:], func=ACT.Copy, bias=0.75)
+            nc.vector.tensor_tensor(turns[:], turns[:], whole[:].bitcast(I32), ALU.subtract)
+            score = ring.tile([P, BANK], F32, name="score", bufs=n_tiles * halves)
+            nc.scalar.activation(out=score[:], in_=turns[:], func=ACT.Sin, scale=-2.0 * math.pi, bias=-1.5 * math.pi)
+            return score
+
+        for b in range(r_passes):
+            for h in range(halves):
+                quantise_placed(b, h)
+        merged = [merge(0, h) for h in range(halves)]
+        for h in range(halves):
+            quantise(z_codes[0][h][:], z_scales[0][h][:], merged[h][:])
+        scores = [[sine(nt, h) for nt in range(n_tiles)] for h in range(halves)]
+        merged = [merge(1, h) for h in range(halves)]
+        for h in range(halves):
+            quantise(z_codes[1][h][:], z_scales[1][h][:], merged[h][:])
+        for h in range(halves):
+            for nt in range(n_tiles):
+                y = second_stage("y", w3_codes, w3_scales, z_codes, z_scales, nt, h)
+                score = scores[h][nt]
+                nc.vector.tensor_tensor(score[:], y[:], score[:], ALU.add)
+                nc.sync.dma_start(out=out[nt * P : (nt + 1) * P, h * BANK : (h + 1) * BANK], in_=score[:])

@@ -23,6 +23,8 @@ PASS = P * PACK
 BANK = 512
 QUADS = 4
 LINE = 4
+PAGES = 2
+ADDS_AFTER_SLICE = (0, 2, 1, 2, 1, 2, 1, 1)
 
 
 def tile_list_song_rotation_scorer_kernel(
@@ -70,7 +72,7 @@ def tile_list_song_rotation_scorer_kernel(
         tab2_planes = zeroed_planes("tab2_planes", 2, T2)
         tab_planes = zeroed_planes("tab_planes", 1, T)
         w4_planes = zeroed_planes("w4_planes", r_passes, N)
-        pages = [keep.tile([P, S], F32, name=f"page{t}") for t in range(PACK)]
+        pages = [keep.tile([P, S], F32, name=f"page{u}") for u in range(PAGES)]
         for page in pages:
             nc.vector.memset(page[:], 0.0)
 
@@ -92,7 +94,7 @@ def tile_list_song_rotation_scorer_kernel(
         nc.sync.dma_start(idx[:], offs)
         tab_w = load_words("tab_w", tab_words[0])
         load_scale_rows(tab_planes, tab_scales)
-        w1_raw = ring.tile([P, PACK, H], F32, name="w1_raw", tag="rows16k")
+        w1_raw = keep.tile([P, PACK, H], F32, name="w1_raw", tag="w1_then_placed")
         nc.sync.dma_start(out=w1_raw[:], in_=w1.rearrange("(p j) c -> p j c", j=PACK))
         feats = []
         for b in range(r_passes):
@@ -134,51 +136,71 @@ def tile_list_song_rotation_scorer_kernel(
                 )
                 quantise(w1_codes[:, cols], w1_scales[:, cols], grouped[:])
 
-        placed = []
-        for b in range(r_passes):
-            if b == 1:
-                quantise_w1()
-            placed_b = ring.tile([P, PACK, S], F32, name=f"placed{b}", tag="rows16k")
-            placed.append(placed_b)
-            for t in range(PACK):
-                cols = slice(b * PASS + t * P, b * PASS + (t + 1) * P)
-                x = psum.tile([P, PICKS], F32, name="x")
-                for a in range(2):
-                    nc.tensor.matmul_mx(
-                        out=x[:],
-                        lhsT=w2_codes[:, a, cols].bitcast(FP4X4),
-                        lhsT_scale=w2_dealt[:, a, cols],
-                        rhs=v2_codes[:, a, :].bitcast(FP8X4),
-                        rhs_scale=v2_scales[:, a, :],
-                        start=(a == 0),
-                        stop=(a == 1),
-                    )
-                act = ring.tile([P, PICKS], F32, name="act", bufs=3)
-                nc.scalar.activation(out=act[:], in_=x[:], func=ACT.Gelu_apprx_tanh)
-                nc.vector.tensor_tensor(pages[t][:].indirect(slots[:]), act[:], weights[:, t, :], ALU.mult)
-                nc.scalar.activation(out=placed_b[:, t, :], in_=pages[t][:], func=ACT.Copy, scale=gains[:, b, t : t + 1])
+        slices = [(b, t) for b in range(r_passes) for t in range(PACK)]
+        acts = []
+        for b, t in slices:
+            cols = slice(b * PASS + t * P, b * PASS + (t + 1) * P)
+            x = psum.tile([P, PICKS], F32, name="x")
+            for a in range(2):
+                nc.tensor.matmul_mx(
+                    out=x[:],
+                    lhsT=w2_codes[:, a, cols].bitcast(FP4X4),
+                    lhsT_scale=w2_dealt[:, a, cols],
+                    rhs=v2_codes[:, a, :].bitcast(FP8X4),
+                    rhs_scale=v2_scales[:, a, :],
+                    start=(a == 0),
+                    stop=(a == 1),
+                )
+            act = ring.tile([P, PICKS], F32, name="act", tag="cols512", bufs=len(slices))
+            nc.scalar.activation(out=act[:], in_=x[:], func=ACT.Gelu_apprx_tanh)
+            nc.gpsimd.tensor_tensor(act[:], act[:], weights[:, t, :], ALU.mult)
+            acts.append(act)
 
         v_codes = keep.tile([P, S], U32, name="v_codes", align_bytes=64)
         v_scales = keep.tile([P, S], U8, name="v_scales", align_bytes=64)
         nc.vector.tensor_copy(v_codes[:], tab_w[:].bitcast(U32).indirect(idx[:]))
         nc.vector.tensor_copy(v_scales[:], tab_planes[:, 0, :].indirect(idx[:]))
+        quantise_w1()
 
-        for b in range(r_passes):
-            for h in range(halves):
-                for t in range(PACK):
-                    cols = slice(b * PASS + t * P, b * PASS + (t + 1) * P)
-                    js = slice(h * BANK, (h + 1) * BANK)
-                    acc = psum.tile([P, BANK], F32, name="acc")
-                    nc.tensor.matmul_mx(
-                        out=acc[:],
-                        lhsT=w1_codes[:, cols].bitcast(FP8X4),
-                        lhsT_scale=w1_scales[:, cols],
-                        rhs=v_codes[:, js].bitcast(FP8X4),
-                        rhs_scale=v_scales[:, js],
-                        start=True,
-                        stop=True,
-                    )
-                    nc.vector.tensor_tensor(feats[b][:, t, js], acc[:], feats[b][:, t, js], ALU.add)
+        def first_product(b, h, t):
+            cols = slice(b * PASS + t * P, b * PASS + (t + 1) * P)
+            js = slice(h * BANK, (h + 1) * BANK)
+            acc = psum.tile([P, BANK], F32, name="acc")
+            nc.tensor.matmul_mx(
+                out=acc[:],
+                lhsT=w1_codes[:, cols].bitcast(FP8X4),
+                lhsT_scale=w1_scales[:, cols],
+                rhs=v_codes[:, js].bitcast(FP8X4),
+                rhs_scale=v_scales[:, js],
+                start=True,
+                stop=True,
+            )
+            return acc, feats[b][:, t, js]
+
+        def add_on_gpsimd(b, h, t):
+            acc, feat = first_product(b, h, t)
+            staged = ring.tile([P, BANK], F32, name="staged", bufs=3)
+            nc.scalar.copy(out=staged[:], in_=acc[:])
+            nc.gpsimd.tensor_tensor(feat, staged[:], feat, ALU.add)
+
+        def add_on_vector(b, h, t):
+            acc, feat = first_product(b, h, t)
+            nc.vector.tensor_tensor(feat, acc[:], feat, ALU.add)
+
+        banks = [(b, h, t) for b in range(r_passes) for h in range(halves) for t in range(PACK)]
+        placed = [
+            keep.tile([P, PACK, S], F32, name="placed0", tag="w1_then_placed"),
+            keep.tile([P, PACK, S], F32, name="placed1"),
+        ]
+        for s, (b, t) in enumerate(slices):
+            page = pages[s % PAGES]
+            nc.vector.tensor_copy(page[:].indirect(slots[:]), acts[s][:])
+            nc.gpsimd.tensor_scalar(placed[b][:, t, :], page[:], gains[:, b, t : t + 1], 0.0, ALU.mult, ALU.add)
+            done = sum(ADDS_AFTER_SLICE[:s])
+            for bank in banks[done : done + ADDS_AFTER_SLICE[s]]:
+                add_on_gpsimd(*bank)
+        for bank in banks[sum(ADDS_AFTER_SLICE) :]:
+            add_on_vector(*bank)
 
         w3_codes = keep.tile([P, r_passes, N], U32, name="w3_codes", align_bytes=64)
         w3_scales = keep.tile([P, r_passes, N], U8, name="w3_scales", align_bytes=64)
@@ -232,7 +254,7 @@ def tile_list_song_rotation_scorer_kernel(
             whole = ring.tile([P, BANK], U32, name="whole")
             nc.scalar.activation(out=whole[:], in_=turns[:], func=ACT.Copy, bias=0.75)
             nc.vector.tensor_tensor(turns[:], turns[:], whole[:].bitcast(I32), ALU.subtract)
-            score = ring.tile([P, BANK], F32, name="score", bufs=n_tiles * halves)
+            score = ring.tile([P, BANK], F32, name="score", tag="cols512", bufs=len(slices))
             nc.scalar.activation(out=score[:], in_=turns[:], func=ACT.Sin, scale=-2.0 * math.pi, bias=-1.5 * math.pi)
             return score
 

@@ -24,7 +24,7 @@ BANK = 512
 QUADS = 4
 LINE = 4
 PAGES = 2
-ADDS_AFTER_SLICE = (0, 2, 1, 2, 1, 2, 1, 1)
+ADDS_AFTER_SLICE = (0, 6, 0, 2, 3, 2, 0, 0)
 
 
 def tile_list_song_rotation_scorer_kernel(
@@ -83,19 +83,23 @@ def tile_list_song_rotation_scorer_kernel(
         load_scale_rows(w2_planes, w2_scales)
         tab2_w = [load_words(f"tab2_w{a}", tab2_words[a]) for a in range(2)]
         load_scale_rows(tab2_planes, tab2_scales)
+        idx = keep.tile([P, S // 16], U16, name="idx")
+        nc.sync.dma_start(idx[:], offs)
+        load_scale_rows(tab_planes, tab_scales)
         slots = keep.tile([P, PICKS // 16], U16, name="slots")
         nc.sync.dma_start(slots[:], pos1)
         weights = keep.tile([P, PACK, PICKS], F32, name="weights")
         for q in range(QUADS):
             nc.sync.dma_start(out=weights[32 * q : 32 * q + 32, :, :], in_=wgs.rearrange("(p t) j -> p t j", t=PACK))
+        tab_w = load_words("tab_w", tab_words[0])
         gains = keep.tile([P, r_passes, PACK], F32, name="gains")
         nc.sync.dma_start(out=gains[:], in_=gain.rearrange("(b p t) -> p b t", p=P, t=PACK))
-        idx = keep.tile([P, S // 16], U16, name="idx")
-        nc.sync.dma_start(idx[:], offs)
-        tab_w = load_words("tab_w", tab_words[0])
-        load_scale_rows(tab_planes, tab_scales)
-        w1_raw = keep.tile([P, PACK, H], F32, name="w1_raw", tag="w1_then_placed")
-        nc.sync.dma_start(out=w1_raw[:], in_=w1.rearrange("(p j) c -> p j c", j=PACK))
+        placed = [keep.tile([P, PACK, S], F32, name=f"placed{b}") for b in range(r_passes)]
+        w1_raw = [
+            placed[b][:, 2 * b : 2 * b + 2, :].rearrange("p u (v c) -> p (u v) c", c=PASS) for b in range(r_passes)
+        ]
+        for b in range(r_passes):
+            nc.sync.dma_start(out=w1_raw[b], in_=w1[:, b * PASS : (b + 1) * PASS].rearrange("(p j) c -> p j c", j=PACK))
         feats = []
         for b in range(r_passes):
             feat = keep.tile([P, PACK, S], F32, name=f"feat{b}")
@@ -107,13 +111,13 @@ def tile_list_song_rotation_scorer_kernel(
 
         w2_codes = keep.tile([P, 2, H], U16, name="w2_codes", align_bytes=64)
         nc.vector.tensor_copy(
-            out=w2_codes[:].rearrange("p a (b t m) -> p (a b) m t", t=PACK, m=P),
-            in_=w2_raw[:].rearrange("p a (b m t) -> p (a b) m t", t=PACK, m=P),
+            out=w2_codes[:].rearrange("p a (b t m) -> p (a b) t m", t=PACK, m=P),
+            in_=w2_raw[:].rearrange("p a (b m t) -> p (a b) t m", t=PACK, m=P),
         )
         w2_dealt = keep.tile([P, 2, H], U8, name="w2_dealt", align_bytes=64)
         nc.vector.tensor_copy(
-            out=w2_dealt[:].rearrange("p a (b t m) -> p (a b) m t", t=PACK, m=P),
-            in_=w2_planes[:].rearrange("p a (b m t) -> p (a b) m t", t=PACK, m=P),
+            out=w2_dealt[:].rearrange("p a (b t m) -> p (a b) t m", t=PACK, m=P),
+            in_=w2_planes[:].rearrange("p a (b m t) -> p (a b) t m", t=PACK, m=P),
         )
 
         v2_codes = keep.tile([P, 2, PICKS], U32, name="v2_codes", align_bytes=64)
@@ -126,15 +130,14 @@ def tile_list_song_rotation_scorer_kernel(
         w1_codes = keep.tile([P, H], U32, name="w1_codes", align_bytes=64)
         w1_scales = keep.tile([P, H], U8, name="w1_scales", align_bytes=64)
 
-        def quantise_w1():
-            for b in range(r_passes):
-                cols = slice(b * PASS, (b + 1) * PASS)
-                grouped = ring.tile([P, PACK * BANK], BF16, name="grouped", bufs=4, align_bytes=64)
-                nc.scalar.copy(
-                    out=grouped[:].rearrange("p (t m j) -> p m j t", t=PACK, j=PACK),
-                    in_=w1_raw[:, :, cols].rearrange("p j (m t) -> p m j t", t=PACK),
-                )
-                quantise(w1_codes[:, cols], w1_scales[:, cols], grouped[:])
+        def quantise_w1(b):
+            cols = slice(b * PASS, (b + 1) * PASS)
+            grouped = ring.tile([P, PACK * BANK], BF16, name="grouped", bufs=4, align_bytes=64)
+            nc.scalar.copy(
+                out=grouped[:].rearrange("p (t m j) -> p m j t", t=PACK, j=PACK),
+                in_=w1_raw[b].rearrange("p j (m t) -> p m j t", t=PACK),
+            )
+            quantise(w1_codes[:, cols], w1_scales[:, cols], grouped[:])
 
         slices = [(b, t) for b in range(r_passes) for t in range(PACK)]
         acts = []
@@ -158,9 +161,9 @@ def tile_list_song_rotation_scorer_kernel(
 
         v_codes = keep.tile([P, S], U32, name="v_codes", align_bytes=64)
         v_scales = keep.tile([P, S], U8, name="v_scales", align_bytes=64)
-        nc.vector.tensor_copy(v_codes[:], tab_w[:].bitcast(U32).indirect(idx[:]))
         nc.vector.tensor_copy(v_scales[:], tab_planes[:, 0, :].indirect(idx[:]))
-        quantise_w1()
+        nc.vector.tensor_copy(v_codes[:], tab_w[:].bitcast(U32).indirect(idx[:]))
+        quantise_w1(0)
 
         def first_product(b, h, t):
             cols = slice(b * PASS + t * P, b * PASS + (t + 1) * P)
@@ -177,40 +180,68 @@ def tile_list_song_rotation_scorer_kernel(
             )
             return acc, feats[b][:, t, js]
 
-        def add_on_gpsimd(b, h, t):
+        stage_tags = ("stage_then_w3", "stage_then_placed", "stage_then_merged")
+        stages = [keep.tile([P, 2, BANK], F32, name=f"stage{u}", tag=tag, align_bytes=64) for u, tag in enumerate(stage_tags)]
+
+        def add_on_gpsimd(i, b, h, t):
             acc, feat = first_product(b, h, t)
-            staged = ring.tile([P, BANK], F32, name="staged", bufs=3)
-            nc.scalar.copy(out=staged[:], in_=acc[:])
-            nc.gpsimd.tensor_tensor(feat, staged[:], feat, ALU.add)
+            staged = staging[i]
+            nc.scalar.copy(out=staged, in_=acc[:])
+            nc.gpsimd.tensor_tensor(feat, staged, feat, ALU.add)
 
         def add_on_vector(b, h, t):
             acc, feat = first_product(b, h, t)
             nc.vector.tensor_tensor(feat, acc[:], feat, ALU.add)
 
+        w3_raw = []
+        for b in range(r_passes):
+            raw = keep.tile([P, PACK, N], F32, name=f"w3_raw{b}")
+            nc.sync.dma_start(out=raw[:], in_=w3[b * PASS : (b + 1) * PASS, :].rearrange("(p t) n -> p t n", t=PACK))
+            w3_raw.append(raw)
+
+        def grouped_tile():
+            return ring.tile([P, PACK * BANK], BF16, name="grouped", bufs=4, align_bytes=64)
+
+        def round_w3(b):
+            grouped = grouped_tile()
+            nc.scalar.copy(out=woven(grouped[:, : PACK * N]), in_=by_rows(w3_raw[b][:]))
+            return grouped
+
+        def round_placed(grouped, b, h, part):
+            lo, hi = part * BANK // 2, (part + 1) * BANK // 2
+            nc.scalar.copy(
+                out=woven(grouped[:, PACK * lo : PACK * hi]),
+                in_=by_rows(placed[b][:, :, h * BANK + lo : h * BANK + hi]),
+            )
+
+        def round_placed_half(b, h):
+            grouped = grouped_tile()
+            for part in range(2):
+                round_placed(grouped, b, h, part)
+            return grouped
+
         banks = [(b, h, t) for b in range(r_passes) for h in range(halves) for t in range(PACK)]
-        placed = [
-            keep.tile([P, PACK, S], F32, name="placed0", tag="w1_then_placed"),
-            keep.tile([P, PACK, S], F32, name="placed1"),
-        ]
+        rows = [placed[1][:, t, h * BANK : (h + 1) * BANK] for t in range(PACK) for h in range(halves)]
+        spare = [stages[i][:, u, :] for u in range(2) for i in (1, 2, 0)]
+        staging = rows[:4] + spare[:2] + rows[4:] + spare[2:]
         for s, (b, t) in enumerate(slices):
             page = pages[s % PAGES]
+            if s == 3:
+                quantise_w1(1)
             nc.vector.tensor_copy(page[:].indirect(slots[:]), acts[s][:])
-            nc.gpsimd.tensor_scalar(placed[b][:, t, :], page[:], gains[:, b, t : t + 1], 0.0, ALU.mult, ALU.add)
+            nc.scalar.activation(out=placed[b][:, t, :], in_=page[:], func=ACT.Copy, scale=gains[:, b, t : t + 1])
             done = sum(ADDS_AFTER_SLICE[:s])
-            for bank in banks[done : done + ADDS_AFTER_SLICE[s]]:
-                add_on_gpsimd(*bank)
+            for i in range(done, done + ADDS_AFTER_SLICE[s]):
+                add_on_gpsimd(i, *banks[i])
+            if s == 3:
+                placed_00 = grouped_tile()
+                round_placed(placed_00, 0, 0, 0)
+            if s == 5:
+                round_placed(placed_00, 0, 0, 1)
+            if s == 6:
+                w3_0 = round_w3(0)
         for bank in banks[sum(ADDS_AFTER_SLICE) :]:
             add_on_vector(*bank)
-
-        w3_codes = keep.tile([P, r_passes, N], U32, name="w3_codes", align_bytes=64)
-        w3_scales = keep.tile([P, r_passes, N], U8, name="w3_scales", align_bytes=64)
-        for b in range(r_passes):
-            w3_raw = keep.tile([P, PACK, N], F32, name="w3_raw")
-            nc.sync.dma_start(out=w3_raw[:], in_=w3[b * PASS : (b + 1) * PASS, :].rearrange("(p t) n -> p t n", t=PACK))
-            grouped = ring.tile([P, PACK * BANK], BF16, name="grouped", bufs=4, align_bytes=64)
-            nc.scalar.copy(out=woven(grouped[:, : PACK * N]), in_=by_rows(w3_raw[:]))
-            for lo, hi in ((0, 256), (256, N)):
-                quantise(w3_codes[:, b, lo:hi], w3_scales[:, b, lo:hi], grouped[:, PACK * lo : PACK * hi])
 
         def second_stage(name, w_codes, w_scales, codes, scales, nt, h):
             acc = psum.tile([P, BANK], F32, name=name)
@@ -220,32 +251,43 @@ def tile_list_song_rotation_scorer_kernel(
                     out=acc[:],
                     lhsT=w_codes[:, b, ns].bitcast(FP8X4),
                     lhsT_scale=w_scales[:, b, ns],
-                    rhs=codes[b][h][:].bitcast(FP8X4),
-                    rhs_scale=scales[b][h][:],
+                    rhs=codes[b][:, h, :].bitcast(FP8X4),
+                    rhs_scale=scales[b][:, h, :],
                     start=(b == 0),
                     stop=(b == r_passes - 1),
                 )
             return acc
 
-        def code_tiles(name, dtype):
+        def code_tiles(name, dtype, first_tag):
             return [
-                [keep.tile([P, BANK], dtype, name=f"{name}{b}{h}", align_bytes=64) for h in range(halves)]
-                for b in range(r_passes)
+                keep.tile([P, halves, BANK], dtype, name=f"{name}{b}", tag=tag, align_bytes=64)
+                for b, tag in enumerate((first_tag, f"{name}1"))
             ]
 
-        p_codes, p_scales = code_tiles("p_codes", U32), code_tiles("p_scales", U8)
-        z_codes, z_scales = code_tiles("z_codes", U32), code_tiles("z_scales", U8)
+        p_codes, p_scales = code_tiles("p_codes", U32, stage_tags[1]), code_tiles("p_scales", U8, "p_scales0")
+        z_codes, z_scales = code_tiles("z_codes", U32, "z_codes0"), code_tiles("z_scales", U8, "z_scales0")
 
-        def quantise_placed(b, h):
-            grouped = ring.tile([P, PACK * BANK], BF16, name="grouped", bufs=4, align_bytes=64)
-            nc.scalar.copy(out=woven(grouped[:]), in_=by_rows(placed[b][:, :, h * BANK : (h + 1) * BANK]))
-            quantise(p_codes[b][h][:], p_scales[b][h][:], grouped[:])
+        w3_codes = keep.tile([P, r_passes, N], U32, name="w3_codes", tag=stage_tags[0], align_bytes=64)
+        w3_scales = keep.tile([P, r_passes, N], U8, name="w3_scales", align_bytes=64)
 
-        def merge(b, h):
+        def quantise_w3(b, grouped):
+            for lo, hi in ((0, 256), (256, N)):
+                quantise(w3_codes[:, b, lo:hi], w3_scales[:, b, lo:hi], grouped[:, PACK * lo : PACK * hi])
+
+        def quantise_placed(b, h, grouped):
+            quantise(p_codes[b][:, h, :], p_scales[b][:, h, :], grouped[:])
+
+        def merge(merged, b, h):
             js = slice(h * BANK, (h + 1) * BANK)
-            grouped = ring.tile([P, PACK * BANK], BF16, name="grouped", bufs=4, align_bytes=64)
-            nc.vector.tensor_tensor(woven(grouped[:]), by_rows(feats[b][:, :, js]), by_rows(placed[b][:, :, js]), ALU.max)
-            return grouped
+            nc.vector.tensor_tensor(
+                woven(merged[:, h, :]), by_rows(feats[b][:, :, js]), by_rows(placed[b][:, :, js]), ALU.max
+            )
+
+        def quantise_merged(merged, b, h):
+            quantise(z_codes[b][:, h, :], z_scales[b][:, h, :], merged[:, h, :])
+
+        def merged_tile(b):
+            return keep.tile([P, halves, PACK * BANK], BF16, name=f"merged{b}", tag=stage_tags[2], align_bytes=64)
 
         def sine(nt, h):
             f = second_stage("f", w4_codes, w4_planes, p_codes, p_scales, nt, h)
@@ -258,16 +300,27 @@ def tile_list_song_rotation_scorer_kernel(
             nc.scalar.activation(out=score[:], in_=turns[:], func=ACT.Sin, scale=-2.0 * math.pi, bias=-1.5 * math.pi)
             return score
 
-        for b in range(r_passes):
-            for h in range(halves):
-                quantise_placed(b, h)
-        merged = [merge(0, h) for h in range(halves)]
+        placed_10 = round_placed_half(1, 0)
+        merged = merged_tile(0)
+        merge(merged, 0, 0)
+        quantise_placed(0, 0, placed_00)
+        quantise_placed(1, 0, placed_10)
+        quantise_w3(0, w3_0)
+        placed_01 = round_placed_half(0, 1)
+        placed_11 = round_placed_half(1, 1)
+        merge(merged, 0, 1)
         for h in range(halves):
-            quantise(z_codes[0][h][:], z_scales[0][h][:], merged[h][:])
-        scores = [[sine(nt, h) for nt in range(n_tiles)] for h in range(halves)]
-        merged = [merge(1, h) for h in range(halves)]
+            quantise_merged(merged, 0, h)
+        merged = merged_tile(1)
+        merge(merged, 1, 0)
+        quantise_placed(0, 1, placed_01)
+        quantise_placed(1, 1, placed_11)
+        scores = [[sine(nt, 0) for nt in range(n_tiles)]]
+        quantise_w3(1, round_w3(1))
+        merge(merged, 1, 1)
         for h in range(halves):
-            quantise(z_codes[1][h][:], z_scales[1][h][:], merged[h][:])
+            quantise_merged(merged, 1, h)
+        scores.append([sine(nt, 1) for nt in range(n_tiles)])
         for h in range(halves):
             for nt in range(n_tiles):
                 y = second_stage("y", w3_codes, w3_scales, z_codes, z_scales, nt, h)

@@ -2,6 +2,7 @@ import math
 from contextlib import ExitStack
 
 import concourse.mybir as mybir
+from concourse.masks import make_identity
 
 K, K2, H, N, T, T2, S, PICKS = 512, 1024, 1024, 384, 4096, 2048, 1024, 512
 FLOPS = 2 * (K * H * S + K2 * H * PICKS + 2 * H * N * S)
@@ -24,7 +25,7 @@ BANK = 512
 QUADS = 4
 LINE = 4
 PAGES = 2
-ADDS_AFTER_SLICE = (0, 6, 0, 2, 3, 2, 0, 0)
+ADDS_AFTER_SLICE = (0, 6, 0, 2, 3, 3, 0, 0)
 
 
 def tile_list_song_rotation_scorer_kernel(
@@ -68,8 +69,8 @@ def tile_list_song_rotation_scorer_kernel(
         def by_rows(ap):
             return ap.rearrange("p t (c i) -> p c t i", i=LINE)
 
-        w2_planes = zeroed_planes("w2_planes", 2, H)
         tab2_planes = zeroed_planes("tab2_planes", 2, T2)
+        w2_planes = zeroed_planes("w2_planes", 2, H)
         tab_planes = zeroed_planes("tab_planes", 1, T)
         w4_planes = zeroed_planes("w4_planes", r_passes, N)
         pages = [keep.tile([P, S], F32, name=f"page{u}") for u in range(PAGES)]
@@ -80,17 +81,16 @@ def tile_list_song_rotation_scorer_kernel(
         nc.sync.dma_start(idx2[:], offs2)
         w2_raw = keep.tile([P, 2, H], U16, name="w2_raw", align_bytes=64)
         nc.sync.dma_start(out=w2_raw[:].bitcast(I32), in_=w2_words.rearrange("a p c -> p a c").bitcast(I32))
-        load_scale_rows(w2_planes, w2_scales)
-        tab2_w = [load_words(f"tab2_w{a}", tab2_words[a]) for a in range(2)]
+        wgs_rows = ring.tile([P, PICKS], F32, name="wgs_rows", tag="turns")
+        nc.sync.dma_start(out=wgs_rows[:], in_=wgs)
         load_scale_rows(tab2_planes, tab2_scales)
+        tab2_w = [load_words(f"tab2_w{a}", tab2_words[a]) for a in range(2)]
+        load_scale_rows(w2_planes, w2_scales)
         idx = keep.tile([P, S // 16], U16, name="idx")
         nc.sync.dma_start(idx[:], offs)
         load_scale_rows(tab_planes, tab_scales)
         slots = keep.tile([P, PICKS // 16], U16, name="slots")
         nc.sync.dma_start(slots[:], pos1)
-        weights = keep.tile([P, PACK, PICKS], F32, name="weights")
-        for q in range(QUADS):
-            nc.sync.dma_start(out=weights[32 * q : 32 * q + 32, :, :], in_=wgs.rearrange("(p t) j -> p t j", t=PACK))
         tab_w = load_words("tab_w", tab_words[0])
         gains = keep.tile([P, r_passes, PACK], F32, name="gains")
         nc.sync.dma_start(out=gains[:], in_=gain.rearrange("(b p t) -> p b t", p=P, t=PACK))
@@ -98,34 +98,58 @@ def tile_list_song_rotation_scorer_kernel(
         w1_raw = [
             placed[b][:, 2 * b : 2 * b + 2, :].rearrange("p u (v c) -> p (u v) c", c=PASS) for b in range(r_passes)
         ]
+        feats = [keep.tile([P, PACK, S], F32, name=f"feat{b}") for b in range(r_passes)]
         for b in range(r_passes):
             nc.sync.dma_start(out=w1_raw[b], in_=w1[:, b * PASS : (b + 1) * PASS].rearrange("(p j) c -> p j c", j=PACK))
-        feats = []
-        for b in range(r_passes):
-            feat = keep.tile([P, PACK, S], F32, name=f"feat{b}")
-            nc.sync.dma_start(out=feat[:], in_=res[b * PASS : (b + 1) * PASS, :].rearrange("(p t) j -> p t j", t=PACK))
-            feats.append(feat)
+            for h in range(halves):
+                js = slice(h * BANK, (h + 1) * BANK)
+                nc.sync.dma_start(
+                    out=feats[b][:, :, js], in_=res[b * PASS : (b + 1) * PASS, js].rearrange("(p t) j -> p t j", t=PACK)
+                )
         w4_codes = keep.tile([P, r_passes, N], I32, name="w4_codes", align_bytes=64)
         nc.sync.dma_start(out=w4_codes[:], in_=w4_words.rearrange("a p c i -> p a (c i)").bitcast(I32))
         load_scale_rows(w4_planes, w4_scales)
 
+        stage_tags = ("stage_then_w3", "stage_then_placed", "stage_then_merged")
+        identity = keep.tile([P, P], F32, name="identity")
+        make_identity(nc, identity[:])
+        blocks = PICKS // P
+        turned = psum.tile([P, blocks, P], F32, name="turned", tag="acc")
+        for jb in range(blocks):
+            nc.tensor.transpose(turned[:, jb, :], wgs_rows[:, jb * P : (jb + 1) * P], identity[:])
+        spread = keep.tile([P, PACK, blocks, P], F32, name="spread", tag=stage_tags[2], align_bytes=64)
+        weights = keep.tile([P, PACK, PICKS], F32, name="weights")
+        for t in range(PACK):
+            nc.scalar.copy(
+                out=spread[:, t, :, :].rearrange("p j (g q) -> p j g q", g=QUADS),
+                in_=turned[:].rearrange("p j (q t) -> p j t q", t=PACK)[:, :, t : t + 1, :].broadcast_to([P, blocks, QUADS, 32]),
+            )
+        for t in range(PACK):
+            back = psum.tile([P, PICKS], F32, name="back", tag=("f", "y")[t % 2])
+            for jb in range(blocks):
+                nc.tensor.transpose(back[:, jb * P : (jb + 1) * P], spread[:, t, jb, :], identity[:])
+            nc.scalar.copy(out=weights[:, t, :], in_=back[:])
+
         w2_codes = keep.tile([P, 2, H], U16, name="w2_codes", align_bytes=64)
-        nc.vector.tensor_copy(
-            out=w2_codes[:].rearrange("p a (b t m) -> p (a b) t m", t=PACK, m=P),
-            in_=w2_raw[:].rearrange("p a (b m t) -> p (a b) t m", t=PACK, m=P),
-        )
         w2_dealt = keep.tile([P, 2, H], U8, name="w2_dealt", align_bytes=64)
-        nc.vector.tensor_copy(
-            out=w2_dealt[:].rearrange("p a (b t m) -> p (a b) t m", t=PACK, m=P),
-            in_=w2_planes[:].rearrange("p a (b m t) -> p (a b) t m", t=PACK, m=P),
-        )
+
+        def deal(dealt, natural, b):
+            cols = slice(b * PASS, (b + 1) * PASS)
+            nc.vector.tensor_copy(
+                out=dealt[:, :, cols].rearrange("p a (t m) -> p a t m", t=PACK),
+                in_=natural[:, :, cols].rearrange("p a (m t) -> p a t m", t=PACK),
+            )
 
         v2_codes = keep.tile([P, 2, PICKS], U32, name="v2_codes", align_bytes=64)
         v2_scales = keep.tile([P, 2, PICKS], U8, name="v2_scales", align_bytes=64)
-        for a in range(2):
-            nc.vector.tensor_copy(v2_codes[:, a, :], tab2_w[a][:].bitcast(U32).indirect(idx2[:]))
+        deal(w2_codes, w2_raw, 0)
         for a in range(2):
             nc.vector.tensor_copy(v2_scales[:, a, :], tab2_planes[:, a, :].indirect(idx2[:]))
+        for a in range(2):
+            nc.vector.tensor_copy(v2_codes[:, a, :], tab2_w[a][:].bitcast(U32).indirect(idx2[:]))
+        deal(w2_dealt, w2_planes, 0)
+        deal(w2_codes, w2_raw, 1)
+        deal(w2_dealt, w2_planes, 1)
 
         w1_codes = keep.tile([P, H], U32, name="w1_codes", align_bytes=64)
         w1_scales = keep.tile([P, H], U8, name="w1_scales", align_bytes=64)
@@ -140,8 +164,9 @@ def tile_list_song_rotation_scorer_kernel(
             quantise(w1_codes[:, cols], w1_scales[:, cols], grouped[:])
 
         slices = [(b, t) for b in range(r_passes) for t in range(PACK)]
-        acts = []
-        for b, t in slices:
+        pairs = [ring.tile([P, 2, PICKS], F32, name=f"acts{i}", tag="cols1024", bufs=4) for i in range(len(slices) // 2)]
+        acts = [pair[:, u, :] for pair in pairs for u in range(2)]
+        for s, (b, t) in enumerate(slices):
             cols = slice(b * PASS + t * P, b * PASS + (t + 1) * P)
             x = psum.tile([P, PICKS], F32, name="x")
             for a in range(2):
@@ -154,10 +179,11 @@ def tile_list_song_rotation_scorer_kernel(
                     start=(a == 0),
                     stop=(a == 1),
                 )
-            act = ring.tile([P, PICKS], F32, name="act", tag="cols512", bufs=len(slices))
-            nc.scalar.activation(out=act[:], in_=x[:], func=ACT.Gelu_apprx_tanh)
-            nc.gpsimd.tensor_tensor(act[:], act[:], weights[:, t, :], ALU.mult)
-            acts.append(act)
+            nc.scalar.activation(out=acts[s], in_=x[:], func=ACT.Gelu_apprx_tanh)
+            if s < 2:
+                nc.gpsimd.tensor_tensor(acts[s], acts[s], weights[:, t, :], ALU.mult)
+            elif s % 2 == 1:
+                nc.gpsimd.tensor_tensor(pairs[s // 2][:], pairs[s // 2][:], weights[:, t - 1 : t + 1, :], ALU.mult)
 
         v_codes = keep.tile([P, S], U32, name="v_codes", align_bytes=64)
         v_scales = keep.tile([P, S], U8, name="v_scales", align_bytes=64)
@@ -180,7 +206,6 @@ def tile_list_song_rotation_scorer_kernel(
             )
             return acc, feats[b][:, t, js]
 
-        stage_tags = ("stage_then_w3", "stage_then_placed", "stage_then_merged")
         stages = [keep.tile([P, 2, BANK], F32, name=f"stage{u}", tag=tag, align_bytes=64) for u, tag in enumerate(stage_tags)]
 
         def add_on_gpsimd(i, b, h, t):
@@ -228,7 +253,7 @@ def tile_list_song_rotation_scorer_kernel(
             page = pages[s % PAGES]
             if s == 3:
                 quantise_w1(1)
-            nc.vector.tensor_copy(page[:].indirect(slots[:]), acts[s][:])
+            nc.vector.tensor_copy(page[:].indirect(slots[:]), acts[s])
             nc.scalar.activation(out=placed[b][:, t, :], in_=page[:], func=ACT.Copy, scale=gains[:, b, t : t + 1])
             done = sum(ADDS_AFTER_SLICE[:s])
             for i in range(done, done + ADDS_AFTER_SLICE[s]):
@@ -289,6 +314,8 @@ def tile_list_song_rotation_scorer_kernel(
         def merged_tile(b):
             return keep.tile([P, halves, PACK * BANK], BF16, name=f"merged{b}", tag=stage_tags[2], align_bytes=64)
 
+        scores = [ring.tile([P, halves, BANK], F32, name=f"scores{nt}", tag="cols1024", bufs=4) for nt in range(n_tiles)]
+
         def sine(nt, h):
             f = second_stage("f", w4_codes, w4_planes, p_codes, p_scales, nt, h)
             turns = ring.tile([P, BANK], F32, name="turns")
@@ -296,9 +323,7 @@ def tile_list_song_rotation_scorer_kernel(
             whole = ring.tile([P, BANK], U32, name="whole")
             nc.scalar.activation(out=whole[:], in_=turns[:], func=ACT.Copy, bias=0.75)
             nc.vector.tensor_tensor(turns[:], turns[:], whole[:].bitcast(I32), ALU.subtract)
-            score = ring.tile([P, BANK], F32, name="score", tag="cols512", bufs=len(slices))
-            nc.scalar.activation(out=score[:], in_=turns[:], func=ACT.Sin, scale=-2.0 * math.pi, bias=-1.5 * math.pi)
-            return score
+            nc.scalar.activation(out=scores[nt][:, h, :], in_=turns[:], func=ACT.Sin, scale=-2.0 * math.pi, bias=-1.5 * math.pi)
 
         placed_10 = round_placed_half(1, 0)
         merged = merged_tile(0)
@@ -311,19 +336,25 @@ def tile_list_song_rotation_scorer_kernel(
         merge(merged, 0, 1)
         for h in range(halves):
             quantise_merged(merged, 0, h)
+
+        def finish(h):
+            for nt in range(n_tiles):
+                y = second_stage("y", w3_codes, w3_scales, z_codes, z_scales, nt, h)
+                score = scores[nt][:, h, :]
+                nc.vector.tensor_tensor(score, y[:], score, ALU.add)
+                nc.sync.dma_start(out=out[nt * P : (nt + 1) * P, h * BANK : (h + 1) * BANK], in_=score)
+
         merged = merged_tile(1)
         merge(merged, 1, 0)
         quantise_placed(0, 1, placed_01)
         quantise_placed(1, 1, placed_11)
-        scores = [[sine(nt, 0) for nt in range(n_tiles)]]
+        quantise_merged(merged, 1, 0)
+        for nt in range(n_tiles):
+            sine(nt, 0)
         quantise_w3(1, round_w3(1))
         merge(merged, 1, 1)
+        for nt in range(n_tiles):
+            sine(nt, 1)
+        quantise_merged(merged, 1, 1)
         for h in range(halves):
-            quantise_merged(merged, 1, h)
-        scores.append([sine(nt, 1) for nt in range(n_tiles)])
-        for h in range(halves):
-            for nt in range(n_tiles):
-                y = second_stage("y", w3_codes, w3_scales, z_codes, z_scales, nt, h)
-                score = scores[h][nt]
-                nc.vector.tensor_tensor(score[:], y[:], score[:], ALU.add)
-                nc.sync.dma_start(out=out[nt * P : (nt + 1) * P, h * BANK : (h + 1) * BANK], in_=score[:])
+            finish(h)

import math
from contextlib import ExitStack

import concourse.mybir as mybir
from concourse.masks import make_identity

K, K2, H, N, T, T2, S, PICKS = 512, 1024, 1024, 384, 4096, 2048, 1024, 512
FLOPS = 2 * (K * H * S + K2 * H * PICKS + 2 * H * N * S)

F32 = mybir.dt.float32
BF16 = mybir.dt.bfloat16
I32 = mybir.dt.int32
U32 = mybir.dt.uint32
U16 = mybir.dt.uint16
U8 = mybir.dt.uint8
FP8X4 = mybir.dt.float8_e4m3fn_x4
FP4X4 = mybir.dt.float4_e2m1fn_x4
ALU = mybir.AluOpType
ACT = mybir.ActivationFunctionType

P = 128
PACK = 4
PASS = P * PACK
BANK = 512
QUADS = 4
LINE = 4
PAGES = 2
ADDS_AFTER_SLICE = (0, 6, 0, 2, 3, 3, 0, 0)


def tile_list_song_rotation_scorer_kernel(
    tc, tab_words, tab_scales, tab2_words, tab2_scales, offs, offs2, pos1, w1, res,
    w2_words, w2_scales, gain, wgs, w3, w4_words, w4_scales, out,
):
    nc = tc.nc
    r_passes = H // PASS
    halves = S // BANK
    n_tiles = N // P

    with ExitStack() as ctx:
        keep = ctx.enter_context(tc.tile_pool(name="keep", bufs=1))
        ring = ctx.enter_context(tc.tile_pool(name="ring", bufs=2))
        psum = ctx.enter_context(tc.psum_pool(name="psum", bufs=2))

        def load_scale_rows(planes, scales):
            for q in range(QUADS):
                nc.sync.dma_start(
                    out=planes[32 * q : 32 * q + 4, :, :].bitcast(I32),
                    in_=scales[:, 4 * q : 4 * q + 4, :].rearrange("a r c -> r a c").bitcast(I32),
                )

        def zeroed_planes(name, passes, width):
            planes = keep.tile([P, passes, width], U8, name=name, align_bytes=64)
            nc.vector.memset(planes[:].rearrange("p a c -> p (a c)").bitcast(I32), 0)
            return planes

        def load_words(name, words):
            width = words.shape[1]
            tile = keep.tile([P, width], I32, name=name, align_bytes=64)
            nc.sync.dma_start(out=tile[:], in_=words.rearrange("p c i -> p (c i)").bitcast(I32))
            return tile

        def quantise(codes, scales, grouped):
            nc.vector.quantize_mx(out=codes.bitcast(FP8X4), scales=scales, in_=grouped)

        def woven(ap):
            return ap.rearrange("p (c i t) -> p c t i", i=LINE, t=PACK)

        def by_rows(ap):
            return ap.rearrange("p t (c i) -> p c t i", i=LINE)

        tab2_planes = zeroed_planes("tab2_planes", 2, T2)
        w2_planes = zeroed_planes("w2_planes", 2, H)
        tab_planes = zeroed_planes("tab_planes", 1, T)
        w4_planes = zeroed_planes("w4_planes", r_passes, N)
        pages = [keep.tile([P, S], F32, name=f"page{u}") for u in range(PAGES)]
        for page in pages:
            nc.vector.memset(page[:], 0.0)

        idx2 = keep.tile([P, PICKS // 16], U16, name="idx2")
        nc.sync.dma_start(idx2[:], offs2)
        w2_raw = keep.tile([P, 2, H], U16, name="w2_raw", align_bytes=64)
        nc.sync.dma_start(out=w2_raw[:].bitcast(I32), in_=w2_words.rearrange("a p c -> p a c").bitcast(I32))
        wgs_rows = ring.tile([P, PICKS], F32, name="wgs_rows", tag="turns")
        nc.sync.dma_start(out=wgs_rows[:], in_=wgs)
        load_scale_rows(tab2_planes, tab2_scales)
        tab2_w = [load_words(f"tab2_w{a}", tab2_words[a]) for a in range(2)]
        load_scale_rows(w2_planes, w2_scales)
        idx = keep.tile([P, S // 16], U16, name="idx")
        nc.sync.dma_start(idx[:], offs)
        load_scale_rows(tab_planes, tab_scales)
        slots = keep.tile([P, PICKS // 16], U16, name="slots")
        nc.sync.dma_start(slots[:], pos1)
        tab_w = load_words("tab_w", tab_words[0])
        gains = keep.tile([P, r_passes, PACK], F32, name="gains")
        nc.sync.dma_start(out=gains[:], in_=gain.rearrange("(b p t) -> p b t", p=P, t=PACK))
        placed = [keep.tile([P, PACK, S], F32, name=f"placed{b}") for b in range(r_passes)]
        w1_raw = [
            placed[b][:, 2 * b : 2 * b + 2, :].rearrange("p u (v c) -> p (u v) c", c=PASS) for b in range(r_passes)
        ]
        feats = [keep.tile([P, PACK, S], F32, name=f"feat{b}") for b in range(r_passes)]
        for b in range(r_passes):
            nc.sync.dma_start(out=w1_raw[b], in_=w1[:, b * PASS : (b + 1) * PASS].rearrange("(p j) c -> p j c", j=PACK))
            for h in range(halves):
                js = slice(h * BANK, (h + 1) * BANK)
                nc.sync.dma_start(
                    out=feats[b][:, :, js], in_=res[b * PASS : (b + 1) * PASS, js].rearrange("(p t) j -> p t j", t=PACK)
                )
        w4_codes = keep.tile([P, r_passes, N], I32, name="w4_codes", align_bytes=64)
        nc.sync.dma_start(out=w4_codes[:], in_=w4_words.rearrange("a p c i -> p a (c i)").bitcast(I32))
        load_scale_rows(w4_planes, w4_scales)

        stage_tags = ("stage_then_w3", "stage_then_placed", "stage_then_merged")
        identity = keep.tile([P, P], F32, name="identity")
        make_identity(nc, identity[:])
        blocks = PICKS // P
        turned = psum.tile([P, blocks, P], F32, name="turned", tag="acc")
        for jb in range(blocks):
            nc.tensor.transpose(turned[:, jb, :], wgs_rows[:, jb * P : (jb + 1) * P], identity[:])
        spread = keep.tile([P, PACK, blocks, P], F32, name="spread", tag=stage_tags[2], align_bytes=64)
        weights = keep.tile([P, PACK, PICKS], F32, name="weights")
        for t in range(PACK):
            nc.scalar.copy(
                out=spread[:, t, :, :].rearrange("p j (g q) -> p j g q", g=QUADS),
                in_=turned[:].rearrange("p j (q t) -> p j t q", t=PACK)[:, :, t : t + 1, :].broadcast_to([P, blocks, QUADS, 32]),
            )
        for t in range(PACK):
            back = psum.tile([P, PICKS], F32, name="back", tag=("f", "y")[t % 2])
            for jb in range(blocks):
                nc.tensor.transpose(back[:, jb * P : (jb + 1) * P], spread[:, t, jb, :], identity[:])
            nc.scalar.copy(out=weights[:, t, :], in_=back[:])

        w2_codes = keep.tile([P, 2, H], U16, name="w2_codes", align_bytes=64)
        w2_dealt = keep.tile([P, 2, H], U8, name="w2_dealt", align_bytes=64)

        def deal(dealt, natural, b):
            cols = slice(b * PASS, (b + 1) * PASS)
            nc.vector.tensor_copy(
                out=dealt[:, :, cols].rearrange("p a (t m) -> p a t m", t=PACK),
                in_=natural[:, :, cols].rearrange("p a (m t) -> p a t m", t=PACK),
            )

        v2_codes = keep.tile([P, 2, PICKS], U32, name="v2_codes", align_bytes=64)
        v2_scales = keep.tile([P, 2, PICKS], U8, name="v2_scales", align_bytes=64)
        deal(w2_codes, w2_raw, 0)
        for a in range(2):
            nc.vector.tensor_copy(v2_scales[:, a, :], tab2_planes[:, a, :].indirect(idx2[:]))
        for a in range(2):
            nc.vector.tensor_copy(v2_codes[:, a, :], tab2_w[a][:].bitcast(U32).indirect(idx2[:]))
        deal(w2_dealt, w2_planes, 0)
        deal(w2_codes, w2_raw, 1)
        deal(w2_dealt, w2_planes, 1)

        w1_codes = keep.tile([P, H], U32, name="w1_codes", align_bytes=64)
        w1_scales = keep.tile([P, H], U8, name="w1_scales", align_bytes=64)

        def quantise_w1(b):
            cols = slice(b * PASS, (b + 1) * PASS)
            grouped = ring.tile([P, PACK * BANK], BF16, name="grouped", bufs=4, align_bytes=64)
            nc.scalar.copy(
                out=grouped[:].rearrange("p (t m j) -> p m j t", t=PACK, j=PACK),
                in_=w1_raw[b].rearrange("p j (m t) -> p m j t", t=PACK),
            )
            quantise(w1_codes[:, cols], w1_scales[:, cols], grouped[:])

        slices = [(b, t) for b in range(r_passes) for t in range(PACK)]
        pairs = [ring.tile([P, 2, PICKS], F32, name=f"acts{i}", tag="cols1024", bufs=4) for i in range(len(slices) // 2)]
        acts = [pair[:, u, :] for pair in pairs for u in range(2)]
        for s, (b, t) in enumerate(slices):
            cols = slice(b * PASS + t * P, b * PASS + (t + 1) * P)
            x = psum.tile([P, PICKS], F32, name="x")
            for a in range(2):
                nc.tensor.matmul_mx(
                    out=x[:],
                    lhsT=w2_codes[:, a, cols].bitcast(FP4X4),
                    lhsT_scale=w2_dealt[:, a, cols],
                    rhs=v2_codes[:, a, :].bitcast(FP8X4),
                    rhs_scale=v2_scales[:, a, :],
                    start=(a == 0),
                    stop=(a == 1),
                )
            nc.scalar.activation(out=acts[s], in_=x[:], func=ACT.Gelu_apprx_tanh)
            if s < 2:
                nc.gpsimd.tensor_tensor(acts[s], acts[s], weights[:, t, :], ALU.mult)
            elif s % 2 == 1:
                nc.gpsimd.tensor_tensor(pairs[s // 2][:], pairs[s // 2][:], weights[:, t - 1 : t + 1, :], ALU.mult)

        v_codes = keep.tile([P, S], U32, name="v_codes", align_bytes=64)
        v_scales = keep.tile([P, S], U8, name="v_scales", align_bytes=64)
        nc.vector.tensor_copy(v_scales[:], tab_planes[:, 0, :].indirect(idx[:]))
        nc.vector.tensor_copy(v_codes[:], tab_w[:].bitcast(U32).indirect(idx[:]))
        quantise_w1(0)

        def first_product(b, h, t):
            cols = slice(b * PASS + t * P, b * PASS + (t + 1) * P)
            js = slice(h * BANK, (h + 1) * BANK)
            acc = psum.tile([P, BANK], F32, name="acc")
            nc.tensor.matmul_mx(
                out=acc[:],
                lhsT=w1_codes[:, cols].bitcast(FP8X4),
                lhsT_scale=w1_scales[:, cols],
                rhs=v_codes[:, js].bitcast(FP8X4),
                rhs_scale=v_scales[:, js],
                start=True,
                stop=True,
            )
            return acc, feats[b][:, t, js]

        stages = [keep.tile([P, 2, BANK], F32, name=f"stage{u}", tag=tag, align_bytes=64) for u, tag in enumerate(stage_tags)]

        def add_on_gpsimd(i, b, h, t):
            acc, feat = first_product(b, h, t)
            staged = staging[i]
            nc.scalar.copy(out=staged, in_=acc[:])
            nc.gpsimd.tensor_tensor(feat, staged, feat, ALU.add)

        def add_on_vector(b, h, t):
            acc, feat = first_product(b, h, t)
            nc.vector.tensor_tensor(feat, acc[:], feat, ALU.add)

        w3_raw = []
        for b in range(r_passes):
            raw = keep.tile([P, PACK, N], F32, name=f"w3_raw{b}")
            nc.sync.dma_start(out=raw[:], in_=w3[b * PASS : (b + 1) * PASS, :].rearrange("(p t) n -> p t n", t=PACK))
            w3_raw.append(raw)

        def grouped_tile():
            return ring.tile([P, PACK * BANK], BF16, name="grouped", bufs=4, align_bytes=64)

        def round_w3(b):
            grouped = grouped_tile()
            nc.scalar.copy(out=woven(grouped[:, : PACK * N]), in_=by_rows(w3_raw[b][:]))
            return grouped

        def round_placed(grouped, b, h, part):
            lo, hi = part * BANK // 2, (part + 1) * BANK // 2
            nc.scalar.copy(
                out=woven(grouped[:, PACK * lo : PACK * hi]),
                in_=by_rows(placed[b][:, :, h * BANK + lo : h * BANK + hi]),
            )

        def round_placed_half(b, h):
            grouped = grouped_tile()
            for part in range(2):
                round_placed(grouped, b, h, part)
            return grouped

        banks = [(b, h, t) for b in range(r_passes) for h in range(halves) for t in range(PACK)]
        rows = [placed[1][:, t, h * BANK : (h + 1) * BANK] for t in range(PACK) for h in range(halves)]
        spare = [stages[i][:, u, :] for u in range(2) for i in (1, 2, 0)]
        staging = rows[:4] + spare[:2] + rows[4:] + spare[2:]
        for s, (b, t) in enumerate(slices):
            page = pages[s % PAGES]
            if s == 3:
                quantise_w1(1)
            nc.vector.tensor_copy(page[:].indirect(slots[:]), acts[s])
            nc.scalar.activation(out=placed[b][:, t, :], in_=page[:], func=ACT.Copy, scale=gains[:, b, t : t + 1])
            done = sum(ADDS_AFTER_SLICE[:s])
            for i in range(done, done + ADDS_AFTER_SLICE[s]):
                add_on_gpsimd(i, *banks[i])
            if s == 3:
                placed_00 = grouped_tile()
                round_placed(placed_00, 0, 0, 0)
            if s == 5:
                round_placed(placed_00, 0, 0, 1)
            if s == 6:
                w3_0 = round_w3(0)
        for bank in banks[sum(ADDS_AFTER_SLICE) :]:
            add_on_vector(*bank)

        def second_stage(name, w_codes, w_scales, codes, scales, nt, h):
            acc = psum.tile([P, BANK], F32, name=name)
            ns = slice(nt * P, (nt + 1) * P)
            for b in range(r_passes):
                nc.tensor.matmul_mx(
                    out=acc[:],
                    lhsT=w_codes[:, b, ns].bitcast(FP8X4),
                    lhsT_scale=w_scales[:, b, ns],
                    rhs=codes[b][:, h, :].bitcast(FP8X4),
                    rhs_scale=scales[b][:, h, :],
                    start=(b == 0),
                    stop=(b == r_passes - 1),
                )
            return acc

        def code_tiles(name, dtype, first_tag):
            return [
                keep.tile([P, halves, BANK], dtype, name=f"{name}{b}", tag=tag, align_bytes=64)
                for b, tag in enumerate((first_tag, f"{name}1"))
            ]

        p_codes, p_scales = code_tiles("p_codes", U32, stage_tags[1]), code_tiles("p_scales", U8, "p_scales0")
        z_codes, z_scales = code_tiles("z_codes", U32, "z_codes0"), code_tiles("z_scales", U8, "z_scales0")

        w3_codes = keep.tile([P, r_passes, N], U32, name="w3_codes", tag=stage_tags[0], align_bytes=64)
        w3_scales = keep.tile([P, r_passes, N], U8, name="w3_scales", align_bytes=64)

        def quantise_w3(b, grouped):
            for lo, hi in ((0, 256), (256, N)):
                quantise(w3_codes[:, b, lo:hi], w3_scales[:, b, lo:hi], grouped[:, PACK * lo : PACK * hi])

        def quantise_placed(b, h, grouped):
            quantise(p_codes[b][:, h, :], p_scales[b][:, h, :], grouped[:])

        def merge(merged, b, h):
            js = slice(h * BANK, (h + 1) * BANK)
            nc.vector.tensor_tensor(
                woven(merged[:, h, :]), by_rows(feats[b][:, :, js]), by_rows(placed[b][:, :, js]), ALU.max
            )

        def quantise_merged(merged, b, h):
            quantise(z_codes[b][:, h, :], z_scales[b][:, h, :], merged[:, h, :])

        def merged_tile(b):
            return keep.tile([P, halves, PACK * BANK], BF16, name=f"merged{b}", tag=stage_tags[2], align_bytes=64)

        scores = [ring.tile([P, halves, BANK], F32, name=f"scores{nt}", tag="cols1024", bufs=4) for nt in range(n_tiles)]

        def sine(nt, h):
            f = second_stage("f", w4_codes, w4_planes, p_codes, p_scales, nt, h)
            turns = ring.tile([P, BANK], F32, name="turns")
            nc.scalar.activation(out=turns[:], in_=f[:], func=ACT.Abs, scale=1.0 / (2.0 * math.pi), bias=-0.25)
            whole = ring.tile([P, BANK], U32, name="whole")
            nc.scalar.activation(out=whole[:], in_=turns[:], func=ACT.Copy, bias=0.75)
            nc.vector.tensor_tensor(turns[:], turns[:], whole[:].bitcast(I32), ALU.subtract)
            nc.scalar.activation(out=scores[nt][:, h, :], in_=turns[:], func=ACT.Sin, scale=-2.0 * math.pi, bias=-1.5 * math.pi)

        placed_10 = round_placed_half(1, 0)
        merged = merged_tile(0)
        merge(merged, 0, 0)
        quantise_placed(0, 0, placed_00)
        quantise_placed(1, 0, placed_10)
        quantise_w3(0, w3_0)
        placed_01 = round_placed_half(0, 1)
        placed_11 = round_placed_half(1, 1)
        merge(merged, 0, 1)
        for h in range(halves):
            quantise_merged(merged, 0, h)

        def finish(h):
            for nt in range(n_tiles):
                y = second_stage("y", w3_codes, w3_scales, z_codes, z_scales, nt, h)
                score = scores[nt][:, h, :]
                nc.vector.tensor_tensor(score, y[:], score, ALU.add)
                nc.sync.dma_start(out=out[nt * P : (nt + 1) * P, h * BANK : (h + 1) * BANK], in_=score)

        merged = merged_tile(1)
        merge(merged, 1, 0)
        quantise_placed(0, 1, placed_01)
        quantise_placed(1, 1, placed_11)
        quantise_merged(merged, 1, 0)
        for nt in range(n_tiles):
            sine(nt, 0)
        quantise_w3(1, round_w3(1))
        merge(merged, 1, 1)
        for nt in range(n_tiles):
            sine(nt, 1)
        quantise_merged(merged, 1, 1)
        for h in range(halves):
            finish(h)
